import numpy as np
import ml_dtypes


def mxq(x, axis, fmt="e4m3"):
    dtype, down = {"e4m3": (ml_dtypes.float8_e4m3fn, 7), "e5m2": (ml_dtypes.float8_e5m2, 14)}[fmt]
    v = np.moveaxis(np.asarray(x, np.float32).astype(ml_dtypes.bfloat16).astype(np.float64), axis, -1)
    blocks = v.reshape(v.shape[:-1] + (-1, 32))
    amax = np.abs(blocks).max(-1, keepdims=True)
    byte = np.maximum(np.where(amax > 0, np.frexp(amax)[1] - 1 + 127, 0) - down, 1)
    scale = np.exp2(byte - 127.0)
    codes = (blocks / scale).astype(np.float32).astype(dtype).astype(np.float64)
    return np.moveaxis((codes * scale).reshape(v.shape), -1, axis)


WIDE = False


def mx_kscale(k):
    if not WIDE:
        return np.ones(k)
    levels = np.array([10, -10, 5, -5, 0])
    if k % 512:
        return np.exp2(np.random.permutation(np.resize(levels, k // 32))).repeat(32)
    a = np.empty((k // 512, 16))
    for p in range(k // 512):
        a[p, :8] = np.random.permutation(np.resize(levels, 8))
        for g in range(8):
            far = levels[np.abs(levels - a[p, g]) >= 10]
            a[p, g + 8] = far[np.random.randint(len(far))]
    return np.exp2(a.ravel()).repeat(32)


BF16 = ml_dtypes.bfloat16


def bf(x):
    return np.asarray(x, np.float32).astype(BF16)


def f64(x):
    return np.asarray(x).astype(np.float64)


E2M1 = np.array([0.0, 0.5, 1.0, 1.5, 2.0, 3.0, 4.0, 6.0, -0.0, -0.5, -1.0, -1.5, -2.0, -3.0, -4.0, -6.0])


def pack_weight(w, fmt):
    k, n = w.shape
    w = f64(bf(w)).reshape(k // 32, 32, n)
    amax = np.abs(w).max(1)
    if fmt == "e4m3":
        byte = np.frexp(amax)[1] - 1 + 127 - 7
    else:
        mant, ex = np.frexp(amax / 6.0)
        byte = np.where(mant > 0.5, ex, ex - 1) + 127
    byte = np.clip(np.where(amax > 0, byte, 1), 1, 254)
    scaled = (w * np.exp2(127.0 - byte)[:, None, :]).reshape(k, n).astype(np.float32)
    by_word = np.ascontiguousarray(scaled.reshape(k // 512, 128, 4, n).transpose(0, 1, 3, 2))
    if fmt == "e4m3":
        words = by_word.astype(ml_dtypes.float8_e4m3fn).view(np.uint8)
    else:
        c = by_word.astype(ml_dtypes.float4_e2m1fn).view(np.uint8) & 0xF
        words = c[..., 0::2] | (c[..., 1::2] << 4)
    return np.ascontiguousarray(words), np.ascontiguousarray(byte.astype(np.uint8).reshape(k // 512, 16, n))


def unpack_weight(words, scales, fmt):
    g, p, n, _ = words.shape
    if fmt == "e4m3":
        vals = np.ascontiguousarray(words).view(ml_dtypes.float8_e4m3fn).astype(np.float64)
    else:
        nib = np.empty((g, p, n, 4), np.uint8)
        nib[..., 0::2] = words & 0xF
        nib[..., 1::2] = words >> 4
        vals = E2M1[nib]
    vals = vals * np.repeat(np.exp2(scales.astype(np.float64) - 127.0), 8, axis=1)[..., None]
    return vals.transpose(0, 1, 3, 2).reshape(g * 512, n)

E4M3FN = np.array([(-1.0 if i & 128 else 1.0) * ((1.0 + (i & 7) / 8.0) * 2.0 ** (((i >> 3) & 15) - 7) if i & 120 else (i & 7) * 2.0 ** -9) for i in range(256)])


def e4m3fn_bytes(y):
    return np.clip(np.asarray(y, np.float64), -448.0, 448.0).astype(np.float32).astype(ml_dtypes.float8_e4m3fn).view(np.uint8)


def e4m3fn_values(b):
    return E4M3FN[b]


P, N, R, V, W = 512, 1024, 1024, 512, 8
J = R // W


def draw0():
    s, t = mx_kscale(N), mx_kscale(P)
    g = (1.0 + 0.1 * np.random.standard_normal(P)) * t
    g[0] = 4.0 * g[0]
    xr = bf(np.random.standard_normal((P, N)) * s)
    xi = bf(np.random.standard_normal((P, N)) * s)
    hr_words, hr_scales = pack_weight(0.7 * np.random.standard_normal((N, R)) / np.sqrt(N) / s[:, None], "e4m3")
    hi_words, hi_scales = pack_weight(0.7 * np.random.standard_normal((N, R)) / np.sqrt(N) / s[:, None], "e4m3")
    fr_words, fr_scales = pack_weight(0.5 * np.random.standard_normal((P, V)) / np.sqrt(P) / t[:, None], "e4m3")
    fi_words, fi_scales = pack_weight(0.5 * np.random.standard_normal((P, V)) / np.sqrt(P) / t[:, None], "e4m3")
    return {
        "xr": xr,
        "xi": xi,
        "hr_words": hr_words,
        "hr_scales": hr_scales,
        "hi_words": hi_words,
        "hi_scales": hi_scales,
        "g": bf(g),
        "fr_words": fr_words,
        "fr_scales": fr_scales,
        "fi_words": fi_words,
        "fi_scales": fi_scales,
    }


def pulse_difference(a):
    return np.concatenate([a[:1], a[1:] - a[:-1]], axis=0)


def core(xr, xi, hr_words, hr_scales, hi_words, hi_scales, g, fr_words, fr_scales, fi_words, fi_scales):
    xrq, xiq = mxq(f64(xr), 1, "e4m3"), mxq(f64(xi), 1, "e4m3")
    hrq, hiq = unpack_weight(hr_words, hr_scales, "e4m3"), unpack_weight(hi_words, hi_scales, "e4m3")
    ar = (xrq @ hrq) - (xiq @ hiq)
    ai = (xrq @ hiq) + (xiq @ hrq)

    dr = pulse_difference(ar)
    di = pulse_difference(ai)

    gv = f64(g)
    tr = gv[:, None] * dr
    ti = gv[:, None] * di

    trq, tiq = mxq(tr, 0, "e4m3"), mxq(ti, 0, "e4m3")
    frq, fiq = unpack_weight(fr_words, fr_scales, "e4m3"), unpack_weight(fi_words, fi_scales, "e4m3")
    br = (frq.T @ trq) - (fiq.T @ tiq)
    bi = (frq.T @ tiq) + (fiq.T @ trq)

    pw = br * br + bi * bi

    blocks = pw.reshape(V, J, W)
    bm = np.mean(blocks, axis=2)

    c = np.maximum(np.roll(bm, 1, axis=1), np.roll(bm, -1, axis=1))

    out = np.log((blocks + 0.1) / (c[:, :, None] + 0.1))
    return out.reshape(V, R)


def setup_inputs():
    drawn = draw0()
    full = np.asarray(drawn['xr']).astype(np.float64)
    scale = (np.abs(full).reshape(4, 128, 8, 128).max(axis=(1, 3)) / 448.0).astype(np.float32)
    given = {}
    for key, value in drawn.items():
        if key == 'xr':
            given['xr_bytes'] = e4m3fn_bytes(full / np.repeat(np.repeat(scale.astype(np.float64), 128, axis=0), 128, axis=1))
            given['xr_scale'] = scale
        else:
            given[key] = value
    return given


def reference(xr_bytes, xr_scale, xi, hr_words, hr_scales, hi_words, hi_scales, g, fr_words, fr_scales, fi_words, fi_scales):
    return core(e4m3fn_values(xr_bytes) * np.repeat(np.repeat(xr_scale.astype(np.float64), 128, axis=0), 128, axis=1), xi, hr_words, hr_scales, hi_words, hi_scales, g, fr_words, fr_scales, fi_words, fi_scales)

from contextlib import ExitStack

import concourse.mybir as mybir
from concourse.masks import make_identity

P, N, R, V, W = 512, 1024, 1024, 512, 8
FLOPS = 4 * 2 * P * N * R + 4 * 2 * P * V * R

F32 = mybir.dt.float32
BF16 = mybir.dt.bfloat16
U32 = mybir.dt.uint32
I32 = mybir.dt.int32
U8 = mybir.dt.uint8
F8 = mybir.dt.float8_e4m3fn
FP8X4 = mybir.dt.float8_e4m3fn_x4
ALU = mybir.AluOpType
ACT = mybir.ActivationFunctionType
AX = mybir.AxisListType

CHUNKS = [0,128,384,640,896,1024]
NQ = len(CHUNKS) - 1


def tile_pulsedopplermtigreatestofcfarmap_d2p_kernel(
    tc, xr_bytes, xr_scale, xi, hr_words, hr_scales, hi_words, hi_scales, g, fr_words, fr_scales, fi_words, fi_scales, out
):
    nc = tc.nc
    with ExitStack() as ctx:
        keep = ctx.enter_context(tc.tile_pool(name="keep", bufs=1))
        work = ctx.enter_context(tc.tile_pool(name="work", bufs=3))
        ps_a = ctx.enter_context(tc.psum_pool(name="ps_a", bufs=4))
        ps_b = ctx.enter_context(tc.psum_pool(name="ps_b", bufs=4))
        ctx.enter_context(tc.manual_schedule())

        one = keep.tile([128, 1], F32, name="one")
        nc.vector.memset(one[:], 1.0)
        warm = keep.tile([128, 1], F32, name="warm")
        hs = keep.tile([128, R], U8, name="hs", align_bytes=64)
        fs = keep.tile([128, V], U8, name="fs", align_bytes=64)
        ident = keep.tile([128, 128], F32, name="ident")
        nc.vector.memset(hs[:].bitcast(I32), 0)
        nc.vector.memset(fs[:].bitcast(I32), 0)
        make_identity(nc, ident[:])

        sc = keep.tile([128, 8], F32, name="sc")
        for i in range(4):
            nc.scalar.dma_start(out=sc[32 * i : 32 * i + 32, :], in_=xr_scale[i].partition_broadcast(32))
        nc.scalar.activation(out=warm[:], in_=one[:], func=ACT.Ln)

        xrv = xr_bytes.rearrange("(m t) k -> m t k", t=4)
        xiv = xi.rearrange("(m t) k -> m t k", t=4)
        xb, xw, xs = [], [], []
        for pr in range(2):
            first = 1 - pr
            b = keep.tile([128, 2, N], U8, name=f"xb{pr}", align_bytes=64)
            nc.sync.dma_start(out=b[:], in_=xrv[:, first : first + 3 : 2, :])
            s = keep.tile([128, 2, N], BF16, name=f"xs{pr}", align_bytes=64)
            nc.sync.dma_start(out=s[:], in_=xiv[:, first : first + 3 : 2, :])
            w = keep.tile([128, 2, N], BF16, name=f"xw{pr}", align_bytes=64)
            xb.append(b)
            xs.append(s)
            xw.append(w)

        def load_scales(tile, src, groups, base):
            for quad in range(4):
                p0 = 32 * quad + base
                nc.sync.dma_start(
                    out=tile[p0 : p0 + 4 * groups, :].bitcast(I32), in_=src[:, 4 * quad : 4 * quad + 4, :].bitcast(I32)
                )

        hwv = [h.rearrange("g p n t -> p g (n t)") for h in (hr_words, hi_words)]
        hw = {}

        def load_h(lo, hi):
            a, z = CHUNKS[lo], CHUNKS[hi]
            for c in range(2):
                t = keep.tile([128, 2, z - a], U32, name=f"hw{c}_{lo}", align_bytes=64)
                nc.sync.dma_start(out=t[:].bitcast(I32), in_=hwv[c][:, :, 4 * a : 4 * z].bitcast(I32))
                for q in range(lo, hi):
                    hw[c, q] = t[:, :, CHUNKS[q] - a : CHUNKS[q + 1] - a]

        load_scales(hs, hr_scales, 2, 0)
        load_scales(hs, hi_scales, 2, 8)
        load_h(0, 1)
        load_h(1, 2)
        g_sb = keep.tile([128, 4], BF16, name="g_sb")
        nc.sync.dma_start(out=g_sb[:], in_=g.rearrange("(p t) -> p t", t=4))
        load_scales(fs, fr_scales, 1, 0)
        load_scales(fs, fi_scales, 1, 4)
        load_h(2, 3)
        fw = []
        for c, f in enumerate((fr_words, fi_words)):
            t = keep.tile([128, V], U32, name=f"fw{c}", align_bytes=64)
            nc.sync.dma_start(out=t[:].bitcast(I32), in_=f[0].rearrange("p n t -> p (n t)").bitcast(I32))
            fw.append(t)
        load_h(3, NQ)

        cx = {}
        grp = {}

        def widen(eng, pr, s, j):
            sl = slice(128 * j, 128 * j + 128)
            src = xb[pr][:, s, sl].bitcast(F8)
            if eng == "v":
                nc.vector.tensor_scalar(
                    out=xw[pr][:, s, sl], in0=src, scalar1=sc[:, j : j + 1], scalar2=None, op0=ALU.mult
                )
            else:
                nc.scalar.activation(out=xw[pr][:, s, sl], in_=src, func=ACT.Copy, scale=sc[:, j : j + 1])

        def turn(name, pr, engs):
            x = xs[pr] if name == "i" else xw[pr]
            grp[name, pr] = keep.tile([128, 2, 2, 128, 4], BF16, name=f"g{name}{pr}", align_bytes=64)
            for gg in range(2):
                bank = ps_b.tile([128, 2, 2, 128], F32, name="b")
                for s in range(2):
                    words = x[:, s, :].bitcast(F32)
                    for u in range(2):
                        nc.tensor.transpose(bank[:, s, u, :], words[:, 256 * gg + u : 256 * (gg + 1) : 2], ident[:])
                copy = nc.scalar.copy if engs[gg] == "s" else nc.vector.tensor_copy
                copy(
                    out=grp[name, pr][:, gg].rearrange("p s m k -> p s (m k)").bitcast(F32).rearrange("p s (m u) -> p s m u", u=2),
                    in_=bank[:].rearrange("p s u m -> p s m u"),
                )

        def negate(pr):
            grp["n", pr] = keep.tile([128, 2, 2, 128, 4], BF16, name=f"gn{pr}", align_bytes=64)
            nc.vector.tensor_scalar(
                out=grp["n", pr][:].rearrange("p a s m k -> p (a s m k)"),
                in0=grp["i", pr][:].rearrange("p a s m k -> p (a s m k)"),
                scalar1=-1.0,
                scalar2=None,
                op0=ALU.mult,
            )

        def quant(name, pr):
            codes = keep.tile([128, 512], U32, name=f"c{name}{pr}", align_bytes=64)
            scales = keep.tile([128, 512], U8, name=f"s{name}{pr}", align_bytes=64)
            nc.vector.quantize_mx(
                out=codes[:].bitcast(FP8X4), scales=scales[:], in_=grp[name, pr][:].rearrange("p a s m k -> p (a s m k)")
            )
            cx[name, pr] = (codes, scales)

        for pr in range(2):
            for s in range(2):
                for j in range(8):
                    widen("v" if j < [5,8][pr] else "s", pr, s, j)
        turn("i", 0, "ss")
        turn("r", 0, "ss")
        quant("i", 0)
        negate(0)
        quant("r", 0)
        quant("n", 0)
        turn("i", 1, "ss")
        turn("r", 1, "ss")
        quant("i", 1)
        quant("r", 1)
        negate(1)
        quant("n", 1)
        gs = keep.tile([128, 4], F32, name="gs")
        nc.vector.tensor_scalar(out=gs[:, 0:4:2], in0=g_sb[:, 0:4:2], scalar1=-1.0, scalar2=None, op0=ALU.mult)
        nc.vector.tensor_scalar(out=gs[:, 1:4:2], in0=g_sb[:, 1:4:2], scalar1=1.0, scalar2=None, op0=ALU.mult)

        def width(q):
            return CHUNKS[q + 1] - CHUNKS[q]

        def compress(q, t):
            pr, s = (0, t // 2) if t % 2 else (1, t // 2)
            w = width(q)
            bank = ps_a.tile([128, 512], F32, name="a")
            for c, terms in ((1, (("i", 0), ("r", 1))), (0, (("r", 0), ("n", 1)))):
                k = 0
                for name, h in terms:
                    codes, scales = cx[name, pr]
                    for gg in range(2):
                        col = (2 * gg + s) * 128
                        nc.tensor.matmul_mx(
                            out=bank[:, w * c : w * (c + 1)],
                            lhsT=codes[:, col : col + 128].bitcast(FP8X4),
                            lhsT_scale=scales[:, col : col + 128],
                            rhs=hw[h, q][:, gg, :].bitcast(FP8X4),
                            rhs_scale=hs[8 * h + 4 * gg :, CHUNKS[q] : CHUNKS[q + 1]],
                            start=(k == 0),
                            stop=(k == 3),
                        )
                        k += 1
            return bank[:, 0 : 2 * w]

        planes = []
        for i in range(3):
            sp = keep.tile([128, 3, 512], F32, name=f"sp{i}")
            nc.gpsimd.memset(sp[0:1, 0, :], 0.0)
            planes.append(sp)

        st = {}
        tq = {}
        tg = {}

        def phase(q, t):
            w = width(q)
            if t == 3:
                st[q] = (
                    planes[q % 3][:, :, 0 : 2 * w],
                    work.tile([128, 4, 512], F32, name="d")[:, :, 0 : 2 * w],
                    work.tile([128, 4, 512], BF16, name="tp")[:, :, 0 : 2 * w],
                )
            sp, d, tp = st[q]
            bank = compress(q, t)
            if t % 2:
                nc.scalar.copy(out=sp[:, (t + 1) // 2, :], in_=bank)
                if t == 3:
                    nc.sync.dma_start(out=sp[1:113, 0, :], in_=sp[0:112, 2, :])
                    nc.sync.dma_start(out=sp[113:128, 0, :], in_=sp[112:127, 2, :])
            else:
                nc.vector.tensor_tensor(
                    out=d[:, t : t + 2, :],
                    in0=sp[:, t // 2 : t // 2 + 2, :],
                    in1=bank.unsqueeze(1).to_broadcast([128, 2, 2 * w]),
                    op=ALU.subtract,
                )

        def taper(q, t):
            sp, d, tp = st[q]
            nc.scalar.activation(out=tp[:, t, :], in_=d[:, t, :], func=ACT.Copy, scale=gs[:, t : t + 1])

        def interleave(q, c):
            w = width(q)
            if q not in tg:
                tg[q] = work.tile([128, 2, 1024], BF16, name="gb", align_bytes=64)[:, :, 0 : 4 * w]
            nc.vector.tensor_copy(
                out=tg[q][:, c, :].rearrange("p (n t) -> p n t", t=4),
                in_=st[q][2][:, :, w * c : w * (c + 1)].rearrange("p t n -> p n t"),
            )

        def tneg(q):
            w = width(q)
            nb = work.tile([128, 1024], BF16, name="nb", align_bytes=64)[:, 0 : 4 * w]
            tn[q] = nb
            if True:
                nc.scalar.activation(out=nb, in_=tg[q][:, 1, :], func=ACT.Copy, scale=-1.0)
            else:
                nc.vector.tensor_scalar(out=nb, in0=tg[q][:, 1, :], scalar1=-1.0, scalar2=None, op0=ALU.mult)

        def tquant(q, c):
            w = width(q)
            codes = work.tile([128, 256], U32, name=f"tc{c}", align_bytes=64)
            scales = work.tile([128, 256], U8, name=f"ts{c}", align_bytes=64)
            nc.vector.quantize_mx(
                out=codes[:, 0:w].bitcast(FP8X4), scales=scales[:, 0:w], in_=tn[q] if c == 2 else tg[q][:, c, :]
            )
            tq[q, c] = (codes[:, 0:w], scales[:, 0:w])

        tn = {}
        pw = keep.tile([128, 4, R], F32, name="pw")
        bs = keep.tile([128, 4, 130], F32, name="bs")
        sqs = {}

        def filt(q, m):
            w = width(q)
            if (q, m // 2) not in sqs:
                sqs[q, m // 2] = work.tile([128, 2, 2, 256], F32, name="sq")
            cols = slice(128 * m, 128 * m + 128)
            bank = ps_b.tile([128, 2, 256], F32, name="b")
            for c, terms in enumerate((((0, 0), (1, 2)), ((0, 1), (1, 0)))):
                for k, (f, x) in enumerate(terms):
                    codes, scales = tq[q, x]
                    nc.tensor.matmul_mx(
                        out=bank[:, c, 0:w],
                        lhsT=fw[f][:, cols].bitcast(FP8X4),
                        lhsT_scale=fs[4 * f :, cols],
                        rhs=codes.bitcast(FP8X4),
                        rhs_scale=scales,
                        start=(k == 0),
                        stop=(k == 1),
                    )
            nc.scalar.activation(out=sqs[q, m // 2][:, m % 2, :, 0:w], in_=bank[:, :, 0:w], func=ACT.Square)

        def power(q, m0, nm):
            w = width(q)
            sq = sqs[q, m0 // 2][:, m0 % 2 : m0 % 2 + nm]
            nc.vector.scalar_tensor_tensor(
                out=pw[:, m0 : m0 + nm, CHUNKS[q] : CHUNKS[q + 1]],
                in0=sq[:, :, 0, 0:w],
                scalar=0.1,
                in1=sq[:, :, 1, 0:w],
                op0=ALU.add,
                op1=ALU.add,
            )

        def sums(q, m0, nm):
            ms = slice(m0, m0 + nm)
            nc.vector.tensor_reduce(
                out=bs[:, ms, CHUNKS[q] // W : CHUNKS[q + 1] // W],
                in_=pw[:, ms, CHUNKS[q] : CHUNKS[q + 1]].rearrange("p m (j w) -> p m j w", w=W),
                axis=AX.X,
                op=ALU.add,
            )

        outv = out.rearrange("(m p) r -> p m r", p=128)
        bounds = [1] + [CHUNKS[q] // W - 1 for q in range(1, NQ)] + [129]
        ccs, rcs, ras = {}, {}, {}

        def greatest(q, m0, nm):
            ms = slice(m0, m0 + nm)
            j0, nj = bounds[q], bounds[q + 1] - bounds[q]
            c = work.tile([128, 4, 34], F32, name="cc")[:, 0:nm, 0:nj]
            ccs[q, m0] = c
            nc.vector.tensor_max(c, bs[:, ms, j0 - 1 : j0 - 1 + nj], bs[:, ms, j0 + 1 : j0 + 1 + nj])

        def inverse(q, m0, nm):
            nj = bounds[q + 1] - bounds[q]
            rc = work.tile([128, 4, 34], F32, name="rc")[:, 0:nm, 0:nj]
            nc.vector.reciprocal(out=rc, in_=ccs[q, m0])
            for i in range(nm):
                rcs[q, m0 + i] = rc[:, i:]

        def pieces(q):
            j0, nj = bounds[q], bounds[q + 1] - bounds[q]
            p = [(j0, min(nj, 128 - j0), 0)]
            if j0 + nj > 128:
                p.append((0, 1, nj - 1))
            return p

        def ratio(q, m0, nm, eng):
            ra = work.tile([128, 2, 34 * W], F32, name="ra", bufs=4)
            ras[q, m0] = ra
            for j, n, at in pieces(q):
                eng.tensor_tensor(
                    out=ra[:, 0:nm, W * at : W * (at + n)].rearrange("p m (j w) -> p m j w", w=W),
                    in0=pw[:, m0 : m0 + nm, W * j : W * (j + n)].rearrange("p m (j w) -> p m j w", w=W),
                    in1=rcs[q, m0][:, 0:nm, at : at + n].unsqueeze(3).to_broadcast([128, nm, n, W]),
                    op=ALU.mult,
                )

        def logs(q, m0, nm):
            nj = bounds[q + 1] - bounds[q]
            ra = ras[q, m0]
            o = work.tile([128, 2, 34 * W], F32, name="o", bufs=4)
            nc.scalar.activation(out=o[:, 0:nm, 0 : W * nj], in_=ra[:, 0:nm, 0 : W * nj], func=ACT.Ln, scale=float(W))
            for j, n, at in pieces(q):
                nc.sync.dma_start(out=outv[:, m0 : m0 + nm, W * j : W * (j + n)], in_=o[:, 0:nm, W * at : W * (at + n)])

        phase(0, 3)
        phase(0, 1)
        for q in range(NQ + 1):
            if q < NQ:
                phase(q, 2)
                phase(q, 0)
                taper(q, 2)
                taper(q, 3)
            if q + 1 < NQ:
                phase(q + 1, 3)
            if q < NQ:
                taper(q, 0)
                taper(q, 1)
            if q + 1 < NQ:
                phase(q + 1, 1)
            if 3 <= q:
                logs(q - 3, 0, 2)
            if 2 <= q:
                power(q - 2, 0, 2)
                power(q - 2, 2, 2)
            if q < NQ:
                interleave(q, 1)
                interleave(q, 0)
            if 3 <= q:
                logs(q - 3, 2, 2)
            if 2 <= q:
                sums(q - 2, 0, 2)
            if q < NQ:
                tneg(q)
            if 1 <= q:
                for m in range(4):
                    filt(q - 1, m)
            if q < NQ:
                tquant(q, 1)
            if 2 <= q:
                sums(q - 2, 2, 2)
            if q < NQ:
                tquant(q, 0)
            if 2 <= q:
                greatest(q - 2, 0, 4)
            if q < NQ:
                tquant(q, 2)
            if 2 <= q:
                inverse(q - 2, 0, 4)
                if q == 2:
                    nc.vector.tensor_copy(out=bs[:, :, 128:130], in_=bs[:, :, 0:2])
                ratio(q - 2, 0, 2, nc.vector)
                ratio(q - 2, 2, 2, nc.vector)
        q = NQ - 1
        ms = list(range(0, 4, 2))
        for m in ms:
            power(q, m, 2)
        logs(q - 1, 0, 2)
        logs(q - 1, 2, 2)
        for m in ms:
            sums(q, m, 2)
        for m in ms:
            greatest(q, m, 2)
        for m in ms:
            inverse(q, m, 2)
        for m in ms:
            ratio(q, m, 2, nc.vector)
            logs(q, m, 2)
